import numpy as np
import ml_dtypes


def mxq(x, axis, fmt="e4m3"):
    dtype, down = {"e4m3": (ml_dtypes.float8_e4m3fn, 7), "e5m2": (ml_dtypes.float8_e5m2, 14)}[fmt]
    v = np.moveaxis(np.asarray(x, np.float32).astype(ml_dtypes.bfloat16).astype(np.float64), axis, -1)
    blocks = v.reshape(v.shape[:-1] + (-1, 32))
    amax = np.abs(blocks).max(-1, keepdims=True)
    byte = np.maximum(np.where(amax > 0, np.frexp(amax)[1] - 1 + 127, 0) - down, 1)
    scale = np.exp2(byte - 127.0)
    codes = (blocks / scale).astype(np.float32).astype(dtype).astype(np.float64)
    return np.moveaxis((codes * scale).reshape(v.shape), -1, axis)


WIDE = False


def mx_kscale(k):
    if not WIDE:
        return np.ones(k)
    levels = np.array([10, -10, 5, -5, 0])
    if k % 512:
        return np.exp2(np.random.permutation(np.resize(levels, k // 32))).repeat(32)
    a = np.empty((k // 512, 16))
    for p in range(k // 512):
        a[p, :8] = np.random.permutation(np.resize(levels, 8))
        for g in range(8):
            far = levels[np.abs(levels - a[p, g]) >= 10]
            a[p, g + 8] = far[np.random.randint(len(far))]
    return np.exp2(a.ravel()).repeat(32)


def f64(x):
    return np.asarray(x).astype(np.float64)


def striped(idx):
    return np.tile(np.asarray(idx).reshape(-1, 16).T, (8, 1)).astype(np.uint16)


def unstriped(offs):
    return offs[:16].T.reshape(-1).astype(np.int64)


E2M1 = np.array([0.0, 0.5, 1.0, 1.5, 2.0, 3.0, 4.0, 6.0, -0.0, -0.5, -1.0, -1.5, -2.0, -3.0, -4.0, -6.0])


def pack_weight(w, fmt):
    k, n = w.shape
    w = f64(np.asarray(w, np.float32).astype(ml_dtypes.bfloat16)).reshape(k // 32, 32, n)
    amax = np.abs(w).max(1)
    if fmt == "e4m3":
        byte = np.frexp(amax)[1] - 1 + 127 - 7
    else:
        mant, ex = np.frexp(amax / 6.0)
        byte = np.where(mant > 0.5, ex, ex - 1) + 127
    byte = np.clip(np.where(amax > 0, byte, 1), 1, 254)
    scaled = (w * np.exp2(127.0 - byte)[:, None, :]).reshape(k, n).astype(np.float32)
    by_word = np.ascontiguousarray(scaled.reshape(k // 512, 128, 4, n).transpose(0, 1, 3, 2))
    if fmt == "e4m3":
        words = by_word.astype(ml_dtypes.float8_e4m3fn).view(np.uint8)
    else:
        c = by_word.astype(ml_dtypes.float4_e2m1fn).view(np.uint8) & 0xF
        words = (c[..., 0::2] | (c[..., 1::2] << 4)).reshape(k // 512, 128, 2 * n)
    return np.ascontiguousarray(words), np.ascontiguousarray(byte.astype(np.uint8).reshape(k // 512, 16, n))


def unpack_weight(words, scales, fmt):
    g, _, n = scales.shape
    words = np.ascontiguousarray(words).reshape(g, 128, n, -1)
    if fmt == "e4m3":
        vals = words.view(ml_dtypes.float8_e4m3fn).astype(np.float64)
    else:
        nib = np.empty((g, 128, n, 4), np.uint8)
        nib[..., 0::2] = words & 0xF
        nib[..., 1::2] = words >> 4
        vals = E2M1[nib]
    vals = vals * np.repeat(np.exp2(scales.astype(np.float64) - 127.0), 8, axis=1)[..., None]
    return vals.transpose(0, 1, 3, 2).reshape(g * 512, n)


B, N, T, D, DV, NQ = 1, 512, 2048, 1024, 256, 256


def setup_inputs():
    n = np.random.standard_normal
    idx = np.random.permutation(T)[:B * N]
    s = mx_kscale(D)[:, None]
    u = np.ones(T)
    u[idx] = mx_kscale(B * N)
    r = np.random.uniform(0.5, 2.0, T)
    qp = [pack_weight(x, "e4m3") for x in n((B, D, NQ)) * s * (0.60 / np.sqrt(D))]
    k = n((D, T)) / s
    v = n((DV, T)) / (u * r)
    kp = pack_weight(k, "e2m1")
    return {
        "q_words": np.stack([x[0] for x in qp]),
        "q_scales": np.stack([x[1] for x in qp]),
        "k_words": np.ascontiguousarray(kp[0].reshape(D // 1024, 2, 128, T, 2).transpose(0, 2, 3, 1, 4)).reshape(D // 1024, 128, T, 4),
        "k_scales": kp[1],
        "vT": v.astype(np.float32),
        "vs": np.tile(u * r, (128, 1)).astype(np.float32),
        "offs": striped(idx),
    }


def reference(q_words, q_scales, k_words, k_scales, vT, vs, offs):
    idx = unstriped(offs)
    k = unpack_weight(k_words.reshape(D // 1024, 128, T, 2, 2).transpose(0, 3, 1, 2, 4).reshape(D // 512, 128, 2 * T), k_scales, "e2m1")
    v = f64(vT)
    pick = lambda x: x[:, idx].reshape(x.shape[0], B, N).transpose(1, 0, 2)
    q = np.stack([unpack_weight(q_words[b], q_scales[b], "e4m3") for b in range(B)])
    score = q.transpose(0, 2, 1) @ pick(k)
    m = score.max(-1, keepdims=True)
    p = np.exp(score - m)
    total = p.sum(-1, keepdims=True)
    w = p * pick(f64(vs))[:, :1, :]
    y = mxq(w, 2, "e4m3") @ mxq(pick(v).transpose(0, 2, 1), 1, "e4m3")
    y = y / total
    return y

@@ -1,0 +1,161 @@
+from contextlib import ExitStack
+
+import concourse.mybir as mybir
+from concourse.masks import make_identity
+
+F32 = mybir.dt.float32
+BF16 = mybir.dt.bfloat16
+I32 = mybir.dt.int32
+U32 = mybir.dt.uint32
+U16 = mybir.dt.uint16
+U8 = mybir.dt.uint8
+FP8X4 = mybir.dt.float8_e4m3fn_x4
+FP4X4 = mybir.dt.float4_e2m1fn_x4
+ACT = mybir.ActivationFunctionType
+ALU = mybir.AluOpType
+
+P = 128
+NQ, N, T, D, DV = 256, 512, 2048, 1024, 256
+PASSES = D // 512
+QB = NQ // P
+VB = DV // P
+VS_ROW = 16
+
+FLOPS = 2 * NQ * N * D + 2 * NQ * N * DV
+
+
+def tile_attend_qpk_topk_kernel(tc, q_words, q_scales, k_words, k_scales, vT, vs, offs, out):
+    nc = tc.nc
+    with ExitStack() as ctx:
+        sb = ctx.enter_context(tc.tile_pool(name="sb", bufs=1))
+        ps = ctx.enter_context(tc.psum_pool(name="ps", bufs=1))
+
+        offsets = sb.tile([P, N // 16], U16, name="offsets")
+        nc.sync.dma_start(offsets[:], offs)
+
+        ks_pool = sb.tile([P, PASSES, T], U8, name="ks_pool")
+        nc.vector.memset(ks_pool[:].bitcast(I32), 0)
+        qs = sb.tile([P, PASSES, NQ], U8, name="qs", align_bytes=64)
+        nc.vector.memset(qs[:].bitcast(I32), 0)
+        vs_pool = sb.tile([P, T], F32, name="vs_pool", tag="slot_max0")
+        nc.vector.memset(vs_pool[:], 0.0)
+
+        warm = sb.tile([P, 1], F32, name="warm")
+        nc.gpsimd.memset(warm[:], 0.0)
+        warm_out = sb.tile([P, 1], F32, name="warm_out")
+        nc.scalar.activation(warm_out[:], warm[:], ACT.Exp)
+        ident = sb.tile([P, P], F32, name="ident")
+        make_identity(nc, ident[:])
+
+        qw = [sb.tile([P, NQ], U32, name=f"qw{o}", align_bytes=64) for o in range(PASSES)]
+        for o in range(PASSES):
+            nc.sync.dma_start(qw[o][:].bitcast(I32), q_words[0, o].rearrange("p q r -> p (q r)").bitcast(I32))
+        for quad in range(4):
+            nc.sync.dma_start(
+                ks_pool[32 * quad : 32 * quad + 4, :, :].bitcast(I32),
+                k_scales[:, 4 * quad : 4 * quad + 4, :].rearrange("o f t -> f o t").bitcast(I32),
+            )
+        kw_pool = sb.tile([P, T], U32, name="kw_pool")
+        nc.sync.dma_start(kw_pool[:].bitcast(I32), k_words[0].rearrange("p t r -> p (t r)").bitcast(I32))
+        for quad in range(4):
+            nc.sync.dma_start(
+                qs[32 * quad : 32 * quad + 4, :, :].bitcast(I32),
+                q_scales[0, :, 4 * quad : 4 * quad + 4, :].rearrange("o f q -> f o q").bitcast(I32),
+            )
+        nc.sync.dma_start(vs_pool[VS_ROW : VS_ROW + 1, :], vs[0:1, :])
+        v_pool = [
+            sb.tile([P, T], F32, name="v_pool0", tag="slot_max1"),
+            sb.tile([P, T], F32, name="v_pool1", tag="v1_w0", align_bytes=64),
+        ]
+        for h in range(VB):
+            nc.sync.dma_start(v_pool[h][:], vT[h * P : (h + 1) * P, :])
+
+        ks = [sb.tile([P, N], U8, name=f"ks{o}", align_bytes=64) for o in range(PASSES)]
+        for o in range(PASSES):
+            nc.vector.tensor_copy(ks[o][:], ks_pool[:, o, :].indirect(offsets[:]))
+        kw_pairs = sb.tile([P, N], U32, name="kw_pairs", tag="pairs_vs")
+        nc.vector.tensor_copy(kw_pairs[:], kw_pool[:].indirect(offsets[:]))
+        kw = [sb.tile([P, N], U16, name=f"kw{o}", align_bytes=64) for o in range(PASSES)]
+        halves = kw_pairs[:].bitcast(U16).rearrange("p (n o) -> p o n", o=PASSES)
+        for o in range(PASSES):
+            nc.vector.tensor_copy(kw[o][:], halves[:, o, :])
+
+        score = [ps.tile([P, N], F32, name=f"score{b}", tag=f"score_vt{b}") for b in range(QB)]
+        for b in range(QB):
+            for o in range(PASSES):
+                nc.tensor.matmul_mx(
+                    out=score[b][:],
+                    lhsT=qw[o][:, b * P : (b + 1) * P].bitcast(FP8X4),
+                    lhsT_scale=qs[:, o, b * P : (b + 1) * P],
+                    rhs=kw[o][:].bitcast(FP4X4),
+                    rhs_scale=ks[o][:],
+                    start=(o == 0),
+                    stop=(o == PASSES - 1),
+                )
+
+        vs_g = sb.tile([P, N], F32, name="vs_g", tag="pairs_vs")
+        nc.vector.tensor_copy(vs_g[:], vs_pool[:].indirect(offsets[:]))
+        vs_col = sb.tile([P, 4], F32, name="vs_col")
+        nc.scalar.dma_start(vs_col[:], vs_g[VS_ROW : VS_ROW + 1, :].rearrange("r (s t) -> r s t", t=4))
+
+        total = [sb.tile([P, 1], F32, name=f"total{b}") for b in range(QB)]
+        p_t = [ps.tile([P, 4, P], F32, name=f"p_t{b}") for b in range(QB)]
+        v_g = []
+        for b in range(QB):
+            neg_max = sb.tile([P, 1], F32, name=f"neg_max{b}", tag=f"slot_max{b}")
+            nc.vector.tensor_reduce(neg_max[:], score[b][:], mybir.AxisListType.X, ALU.max, negate=True)
+            p = sb.tile([P, 4, P], F32, name=f"p{b}")
+            nc.scalar.activation(
+                p[:], score[b][:].rearrange("q (s t) -> q t s", t=4), ACT.Exp, bias=neg_max[:], accum_out=total[b][:]
+            )
+            for t in range(4):
+                nc.tensor.transpose(p_t[b][:, t, :], p[:, t, :], ident[:])
+            v_g.append(sb.tile([P, N], BF16, name=f"v_g{b}"))
+            nc.vector.tensor_copy(v_g[b][:], v_pool[b][:].indirect(offsets[:]))
+
+        v_codes = sb.tile([P, DV], U32, name="v_codes", align_bytes=64)
+        v_scales = sb.tile([P, DV], U8, name="v_scales", align_bytes=64)
+        v_bf = []
+        for h in range(VB):
+            v_t = ps.tile([P, 2, P], F32, name=f"v_t{h}", tag=f"score_vt{h}")
+            for u in range(2):
+                nc.tensor.transpose(v_t[:, u, :], v_g[h][:].bitcast(F32)[:, u::2], ident[:])
+            v_bf.append(sb.tile([P, P * 4], BF16, name=f"v_bf{h}", align_bytes=64))
+            nc.scalar.copy(v_bf[h][:].bitcast(F32).rearrange("s (e u) -> s e u", u=2), v_t[:].rearrange("s u e -> s e u"))
+        w_all = sb.tile([P, QB, P * 4], BF16, name="w_all", tag="v1_w0", align_bytes=64)
+        w_bf = [w_all[:, b, :] for b in range(QB)]
+        for h in range(QB):
+            nc.vector.tensor_tensor(
+                w_bf[h].rearrange("s (q t) -> s q t", t=4),
+                p_t[h][:].rearrange("s t q -> s q t"),
+                vs_col[:].unsqueeze(1).to_broadcast([P, P, 4]),
+                ALU.mult,
+            )
+
+        w_codes = [sb.tile([P, P], U32, name=f"w_codes{b}", align_bytes=64) for b in range(QB)]
+        w_scales = [sb.tile([P, P], U8, name=f"w_scales{b}", align_bytes=64) for b in range(QB)]
+        inv = [sb.tile([P, 1], F32, name=f"inv{b}") for b in range(QB)]
+        for h in range(VB):
+            nc.vector.quantize_mx(v_codes[:, h * P : (h + 1) * P].bitcast(FP8X4), v_scales[:, h * P : (h + 1) * P], v_bf[h][:])
+        for b in range(QB):
+            nc.vector.reciprocal(inv[b][:], total[b][:])
+            nc.vector.quantize_mx(w_codes[b][:].bitcast(FP8X4), w_scales[b][:], w_bf[b])
+
+        for b in range(QB):
+            y = ps.tile([P, DV], F32, name=f"y{b}")
+            nc.tensor.matmul_mx(
+                out=y[:],
+                lhsT=w_codes[b][:].bitcast(FP8X4),
+                lhsT_scale=w_scales[b][:],
+                rhs=v_codes[:].bitcast(FP8X4),
+                rhs_scale=v_scales[:],
+                start=True,
+                stop=True,
+            )
+            res = sb.tile([P, DV], F32, name=f"res{b}")
+            if b == 0:
+                nc.scalar.activation(res[:], y[:], ACT.Copy, scale=inv[b][:])
+                nc.scalar.dma_start(out[0, b * P : (b + 1) * P, :], res[:])
+            else:
+                nc.vector.tensor_scalar(res[:], y[:], inv[b][:], None, ALU.mult)
+                nc.sync.dma_start(out[0, b * P : (b + 1) * P, :], res[:])

@@ -20,6 +20,7 @@ PASSES = D // 512
 QB = NQ // P
 VB = DV // P
 VS_ROW = 16
+V_HEAD = 768
 
 FLOPS = 2 * NQ * N * D + 2 * NQ * N * DV
 
@@ -28,17 +29,20 @@ def tile_attend_qpk_topk_kernel(tc, q_words, q_scales, k_words, k_scales, vT, vs
     nc = tc.nc
     with ExitStack() as ctx:
         sb = ctx.enter_context(tc.tile_pool(name="sb", bufs=1))
+        late = ctx.enter_context(tc.tile_pool(name="late", bufs=1))
         ps = ctx.enter_context(tc.psum_pool(name="ps", bufs=1))
 
         offsets = sb.tile([P, N // 16], U16, name="offsets")
         nc.sync.dma_start(offsets[:], offs)
 
-        ks_pool = sb.tile([P, PASSES, T], U8, name="ks_pool")
+        ks_pool = sb.tile([P, T], U8, name="ks_pool")
         nc.vector.memset(ks_pool[:].bitcast(I32), 0)
         qs = sb.tile([P, PASSES, NQ], U8, name="qs", align_bytes=64)
         nc.vector.memset(qs[:].bitcast(I32), 0)
-        vs_pool = sb.tile([P, T], F32, name="vs_pool", tag="slot_max0")
+        vs_pool = sb.tile([P, T], F32, name="vs_pool")
         nc.vector.memset(vs_pool[:], 0.0)
+        ks = sb.tile([P, PASSES, N], U8, name="ks", align_bytes=64)
+        nc.vector.memset(ks[:].bitcast(I32), 0)
 
         warm = sb.tile([P, 1], F32, name="warm")
         nc.gpsimd.memset(warm[:], 0.0)
@@ -46,116 +50,128 @@ def tile_attend_qpk_topk_kernel(tc, q_words, q_scales, k_words, k_scales, vT, vs
         nc.scalar.activation(warm_out[:], warm[:], ACT.Exp)
         ident = sb.tile([P, P], F32, name="ident")
         make_identity(nc, ident[:])
+        minus_one = sb.tile([P, 1], F32, name="minus_one")
+        nc.gpsimd.memset(minus_one[:], -1.0)
 
-        qw = [sb.tile([P, NQ], U32, name=f"qw{o}", align_bytes=64) for o in range(PASSES)]
-        for o in range(PASSES):
-            nc.sync.dma_start(qw[o][:].bitcast(I32), q_words[0, o].rearrange("p q r -> p (q r)").bitcast(I32))
-        for quad in range(4):
-            nc.sync.dma_start(
-                ks_pool[32 * quad : 32 * quad + 4, :, :].bitcast(I32),
-                k_scales[:, 4 * quad : 4 * quad + 4, :].rearrange("o f t -> f o t").bitcast(I32),
-            )
-        kw_pool = sb.tile([P, T], U32, name="kw_pool")
-        nc.sync.dma_start(kw_pool[:].bitcast(I32), k_words[0].rearrange("p t r -> p (t r)").bitcast(I32))
+        qw = sb.tile([P, PASSES, NQ], U32, name="qw", align_bytes=64)
+        nc.sync.dma_start(qw[:].bitcast(I32), q_words[0].rearrange("o p q r -> p o (q r)").bitcast(I32))
+        nc.sync.dma_start(ks_pool[0:P:4, :].bitcast(I32), k_scales.rearrange("o f t -> f o t").bitcast(I32))
         for quad in range(4):
             nc.sync.dma_start(
                 qs[32 * quad : 32 * quad + 4, :, :].bitcast(I32),
                 q_scales[0, :, 4 * quad : 4 * quad + 4, :].rearrange("o f q -> f o q").bitcast(I32),
             )
+        kw_pool = sb.tile([P, T], U32, name="kw_pool")
+        kw_dram = k_words[0].rearrange("p t r -> p (t r)").bitcast(I32)
+        nc.sync.dma_start(kw_pool[:, : T // 2].bitcast(I32), kw_dram[:, : T // 2])
         nc.sync.dma_start(vs_pool[VS_ROW : VS_ROW + 1, :], vs[0:1, :])
+        nc.sync.dma_start(kw_pool[:, T // 2 :].bitcast(I32), kw_dram[:, T // 2 :])
         v_pool = [
-            sb.tile([P, T], F32, name="v_pool0", tag="slot_max1"),
-            sb.tile([P, T], F32, name="v_pool1", tag="v1_w0", align_bytes=64),
+            late.tile([P, T], F32, name="v_pool0", offset=0),
+            late.tile([P, T], F32, name="v_pool1", offset=4 * T),
         ]
-        for h in range(VB):
-            nc.sync.dma_start(v_pool[h][:], vT[h * P : (h + 1) * P, :])
+        nc.sync.dma_start(v_pool[0][:, :V_HEAD], vT[0:P, :V_HEAD])
 
-        ks = [sb.tile([P, N], U8, name=f"ks{o}", align_bytes=64) for o in range(PASSES)]
-        for o in range(PASSES):
-            nc.vector.tensor_copy(ks[o][:], ks_pool[:, o, :].indirect(offsets[:]))
-        kw_pairs = sb.tile([P, N], U32, name="kw_pairs", tag="pairs_vs")
+        ks_rows = sb.tile([P, N], U8, name="ks_rows")
+        nc.vector.tensor_copy(ks_rows[:], ks_pool[:].indirect(offsets[:]))
+        for quad in range(4):
+            nc.sync.dma_start(
+                ks[32 * quad : 32 * quad + 4, :, :].bitcast(I32), ks_rows[32 * quad : 32 * quad + 32 : 4, :].bitcast(I32)
+            )
+        nc.sync.dma_start(v_pool[0][:, V_HEAD:], vT[0:P, V_HEAD:])
+        nc.sync.dma_start(v_pool[1][:], vT[P : 2 * P, :])
+
+        vs_g = sb.tile([P, N], F32, name="vs_g")
+        nc.vector.tensor_copy(vs_g[:], vs_pool[:].indirect(offsets[:]))
+        vs_col = sb.tile([P, 4], F32, name="vs_col")
+        nc.scalar.dma_start(vs_col[:], vs_g[VS_ROW : VS_ROW + 1, :].rearrange("r (s t) -> r s t", t=4))
+
+        kw_pairs = sb.tile([P, N], U32, name="kw_pairs")
         nc.vector.tensor_copy(kw_pairs[:], kw_pool[:].indirect(offsets[:]))
         kw = [sb.tile([P, N], U16, name=f"kw{o}", align_bytes=64) for o in range(PASSES)]
         halves = kw_pairs[:].bitcast(U16).rearrange("p (n o) -> p o n", o=PASSES)
         for o in range(PASSES):
             nc.vector.tensor_copy(kw[o][:], halves[:, o, :])
 
-        score = [ps.tile([P, N], F32, name=f"score{b}", tag=f"score_vt{b}") for b in range(QB)]
+        score = [ps.tile([P, N], F32, name=f"score{b}", tag=f"score{b}") for b in range(QB)]
         for b in range(QB):
             for o in range(PASSES):
                 nc.tensor.matmul_mx(
                     out=score[b][:],
-                    lhsT=qw[o][:, b * P : (b + 1) * P].bitcast(FP8X4),
+                    lhsT=qw[:, o, b * P : (b + 1) * P].bitcast(FP8X4),
                     lhsT_scale=qs[:, o, b * P : (b + 1) * P],
                     rhs=kw[o][:].bitcast(FP4X4),
-                    rhs_scale=ks[o][:],
+                    rhs_scale=ks[:, o, :],
                     start=(o == 0),
                     stop=(o == PASSES - 1),
                 )
 
-        vs_g = sb.tile([P, N], F32, name="vs_g", tag="pairs_vs")
-        nc.vector.tensor_copy(vs_g[:], vs_pool[:].indirect(offsets[:]))
-        vs_col = sb.tile([P, 4], F32, name="vs_col")
-        nc.scalar.dma_start(vs_col[:], vs_g[VS_ROW : VS_ROW + 1, :].rearrange("r (s t) -> r s t", t=4))
+        def values(h, bank):
+            v_g = sb.tile([P, N], BF16, name=f"v_g{h}")
+            nc.vector.tensor_copy(v_g[:], v_pool[h][:].indirect(offsets[:]))
+            v_t = ps.tile([P, 2, P], F32, name=f"v_t{h}", tag=bank)
+            for u in range(2):
+                nc.tensor.transpose(v_t[:, u, :], v_g[:].bitcast(F32)[:, u::2], ident[:])
+            v_bf = sb.tile([P, P * 4], BF16, name=f"v_bf{h}", align_bytes=64)
+            nc.scalar.copy(v_bf[:].bitcast(F32).rearrange("s (e u) -> s e u", u=2), v_t[:].rearrange("s u e -> s e u"))
+            return v_bf
 
-        total = [sb.tile([P, 1], F32, name=f"total{b}") for b in range(QB)]
-        p_t = [ps.tile([P, 4, P], F32, name=f"p_t{b}") for b in range(QB)]
-        v_g = []
+        def quantise(src, name):
+            codes = sb.tile([P, P], U32, name=f"{name}_codes", align_bytes=64)
+            scales = sb.tile([P, P], U8, name=f"{name}_scales", align_bytes=64)
+            nc.vector.quantize_mx(codes[:].bitcast(FP8X4), scales[:], src[:])
+            return codes, scales
+
+        v_bf = [values(0, "v_t0")]
+        p_t = []
+        inv = []
         for b in range(QB):
-            neg_max = sb.tile([P, 1], F32, name=f"neg_max{b}", tag=f"slot_max{b}")
+            neg_max = late.tile([P, 1], F32, name=f"neg_max{b}", offset=b * 64)
             nc.vector.tensor_reduce(neg_max[:], score[b][:], mybir.AxisListType.X, ALU.max, negate=True)
             p = sb.tile([P, 4, P], F32, name=f"p{b}")
+            total = sb.tile([P, 1], F32, name=f"total{b}")
             nc.scalar.activation(
-                p[:], score[b][:].rearrange("q (s t) -> q t s", t=4), ACT.Exp, bias=neg_max[:], accum_out=total[b][:]
+                p[:], score[b][:].rearrange("q (s t) -> q t s", t=4), ACT.Exp, bias=neg_max[:], accum_out=total[:]
             )
+            p_t.append(ps.tile([P, 4, P], F32, name=f"p_t{b}"))
             for t in range(4):
                 nc.tensor.transpose(p_t[b][:, t, :], p[:, t, :], ident[:])
-            v_g.append(sb.tile([P, N], BF16, name=f"v_g{b}"))
-            nc.vector.tensor_copy(v_g[b][:], v_pool[b][:].indirect(offsets[:]))
+            inv.append(sb.tile([P, 1], F32, name=f"inv{b}"))
+            nc.gpsimd.tensor_tensor(inv[b][:], total[:], minus_one[:], ALU.pow)
+        v_bf.append(values(1, "score1"))
 
-        v_codes = sb.tile([P, DV], U32, name="v_codes", align_bytes=64)
-        v_scales = sb.tile([P, DV], U8, name="v_scales", align_bytes=64)
-        v_bf = []
-        for h in range(VB):
-            v_t = ps.tile([P, 2, P], F32, name=f"v_t{h}", tag=f"score_vt{h}")
-            for u in range(2):
-                nc.tensor.transpose(v_t[:, u, :], v_g[h][:].bitcast(F32)[:, u::2], ident[:])
-            v_bf.append(sb.tile([P, P * 4], BF16, name=f"v_bf{h}", align_bytes=64))
-            nc.scalar.copy(v_bf[h][:].bitcast(F32).rearrange("s (e u) -> s e u", u=2), v_t[:].rearrange("s u e -> s e u"))
-        w_all = sb.tile([P, QB, P * 4], BF16, name="w_all", tag="v1_w0", align_bytes=64)
-        w_bf = [w_all[:, b, :] for b in range(QB)]
-        for h in range(QB):
+        w_bf = []
+        for b in range(QB):
+            w_bf.append(late.tile([P, P * 4], BF16, name=f"w_bf{b}", offset=4 * T + b * 1024, align_bytes=64))
             nc.vector.tensor_tensor(
-                w_bf[h].rearrange("s (q t) -> s q t", t=4),
-                p_t[h][:].rearrange("s t q -> s q t"),
+                w_bf[b][:].rearrange("s (q t) -> s q t", t=4),
+                p_t[b][:].rearrange("s t q -> s q t"),
                 vs_col[:].unsqueeze(1).to_broadcast([P, P, 4]),
                 ALU.mult,
             )
 
-        w_codes = [sb.tile([P, P], U32, name=f"w_codes{b}", align_bytes=64) for b in range(QB)]
-        w_scales = [sb.tile([P, P], U8, name=f"w_scales{b}", align_bytes=64) for b in range(QB)]
-        inv = [sb.tile([P, 1], F32, name=f"inv{b}") for b in range(QB)]
-        for h in range(VB):
-            nc.vector.quantize_mx(v_codes[:, h * P : (h + 1) * P].bitcast(FP8X4), v_scales[:, h * P : (h + 1) * P], v_bf[h][:])
-        for b in range(QB):
-            nc.vector.reciprocal(inv[b][:], total[b][:])
-            nc.vector.quantize_mx(w_codes[b][:].bitcast(FP8X4), w_scales[b][:], w_bf[b])
+        v_mx = [quantise(v_bf[0], "v0")]
+        w_mx = [quantise(w_bf[b], f"w{b}") for b in range(QB)]
+        v_mx.append(quantise(v_bf[1], "v1"))
 
+        y = [ps.tile([P, VB, P], F32, name=f"y{b}") for b in range(QB)]
+        for h in range(VB):
+            for b in range(QB):
+                nc.tensor.matmul_mx(
+                    out=y[b][:, h, :],
+                    lhsT=w_mx[b][0][:].bitcast(FP8X4),
+                    lhsT_scale=w_mx[b][1][:],
+                    rhs=v_mx[h][0][:].bitcast(FP8X4),
+                    rhs_scale=v_mx[h][1][:],
+                    start=True,
+                    stop=True,
+                )
         for b in range(QB):
-            y = ps.tile([P, DV], F32, name=f"y{b}")
-            nc.tensor.matmul_mx(
-                out=y[:],
-                lhsT=w_codes[b][:].bitcast(FP8X4),
-                lhsT_scale=w_scales[b][:],
-                rhs=v_codes[:].bitcast(FP8X4),
-                rhs_scale=v_scales[:],
-                start=True,
-                stop=True,
-            )
             res = sb.tile([P, DV], F32, name=f"res{b}")
+            y_row = y[b][:].rearrange("q h e -> q (h e)")
             if b == 0:
-                nc.scalar.activation(res[:], y[:], ACT.Copy, scale=inv[b][:])
+                nc.scalar.activation(res[:], y_row, ACT.Copy, scale=inv[b][:])
                 nc.scalar.dma_start(out[0, b * P : (b + 1) * P, :], res[:])
             else:
-                nc.vector.tensor_scalar(res[:], y[:], inv[b][:], None, ALU.mult)
+                nc.vector.tensor_scalar(res[:], y_row, inv[b][:], None, ALU.mult)
                 nc.sync.dma_start(out[0, b * P : (b + 1) * P, :], res[:])

@@ -20,7 +20,7 @@ PASSES = D // 512
 QB = NQ // P
 VB = DV // P
 VS_ROW = 16
-V_HEAD = 768
+V_HEAD = 1024
 
 FLOPS = 2 * NQ * N * D + 2 * NQ * N * DV
 
@@ -129,13 +129,17 @@ def tile_attend_qpk_topk_kernel(tc, q_words, q_scales, k_words, k_scales, vT, vs
             neg_max = late.tile([P, 1], F32, name=f"neg_max{b}", offset=b * 64)
             nc.vector.tensor_reduce(neg_max[:], score[b][:], mybir.AxisListType.X, ALU.max, negate=True)
             p = sb.tile([P, 4, P], F32, name=f"p{b}")
+            sums = sb.tile([P, 2], F32, name=f"sums{b}")
+            dealt = score[b][:].rearrange("q (s t) -> q t s", t=4)
+            p_t.append(ps.tile([P, 4, P], F32, name=f"p_t{b}", tag=f"p_t{b}"))
+            for u in range(2):
+                nc.scalar.activation(
+                    p[:, 2 * u : 2 * u + 2, :], dealt[:, 2 * u : 2 * u + 2, :], ACT.Exp, bias=neg_max[:], accum_out=sums[:, u : u + 1]
+                )
+                for t in range(2 * u, 2 * u + 2):
+                    nc.tensor.transpose(p_t[b][:, t, :], p[:, t, :], ident[:])
             total = sb.tile([P, 1], F32, name=f"total{b}")
-            nc.scalar.activation(
-                p[:], score[b][:].rearrange("q (s t) -> q t s", t=4), ACT.Exp, bias=neg_max[:], accum_out=total[:]
-            )
-            p_t.append(ps.tile([P, 4, P], F32, name=f"p_t{b}"))
-            for t in range(4):
-                nc.tensor.transpose(p_t[b][:, t, :], p[:, t, :], ident[:])
+            nc.gpsimd.tensor_tensor(total[:], sums[:, 0:1], sums[:, 1:2], ALU.add)
             inv.append(sb.tile([P, 1], F32, name=f"inv{b}"))
             nc.gpsimd.tensor_tensor(inv[b][:], total[:], minus_one[:], ALU.pow)
         v_bf.append(values(1, "score1"))
@@ -154,11 +158,11 @@ def tile_attend_qpk_topk_kernel(tc, q_words, q_scales, k_words, k_scales, vT, vs
         w_mx = [quantise(w_bf[b], f"w{b}") for b in range(QB)]
         v_mx.append(quantise(v_bf[1], "v1"))
 
-        y = [ps.tile([P, VB, P], F32, name=f"y{b}") for b in range(QB)]
         for h in range(VB):
             for b in range(QB):
+                y = ps.tile([P, P], F32, name=f"y{b}{h}", tag=f"y{b}" if h == 0 else f"p_t{b}")
                 nc.tensor.matmul_mx(
-                    out=y[b][:, h, :],
+                    out=y[:],
                     lhsT=w_mx[b][0][:].bitcast(FP8X4),
                     lhsT_scale=w_mx[b][1][:],
                     rhs=v_mx[h][0][:].bitcast(FP8X4),
@@ -166,12 +170,11 @@ def tile_attend_qpk_topk_kernel(tc, q_words, q_scales, k_words, k_scales, vT, vs
                     start=True,
                     stop=True,
                 )
-        for b in range(QB):
-            res = sb.tile([P, DV], F32, name=f"res{b}")
-            y_row = y[b][:].rearrange("q h e -> q (h e)")
-            if b == 0:
-                nc.scalar.activation(res[:], y_row, ACT.Copy, scale=inv[b][:])
-                nc.scalar.dma_start(out[0, b * P : (b + 1) * P, :], res[:])
-            else:
-                nc.vector.tensor_scalar(res[:], y_row, inv[b][:], None, ALU.mult)
-                nc.sync.dma_start(out[0, b * P : (b + 1) * P, :], res[:])
+                res = sb.tile([P, P], F32, name=f"res{b}{h}")
+                dst = out[0, b * P : (b + 1) * P, h * P : (h + 1) * P]
+                if (b, h) == (QB - 1, VB - 1):
+                    nc.vector.tensor_scalar(res[:], y[:], inv[b][:], None, ALU.mult)
+                    nc.sync.dma_start(dst, res[:])
+                else:
+                    nc.scalar.activation(res[:], y[:], ACT.Copy, scale=inv[b][:])
+                    (nc.sync if h == 0 else nc.scalar).dma_start(dst, res[:])

@@ -40,7 +40,7 @@ def tile_attend_qpk_topk_kernel(tc, q_words, q_scales, k_words, k_scales, vT, vs
         qs = sb.tile([P, PASSES, NQ], U8, name="qs", align_bytes=64)
         nc.vector.memset(qs[:].bitcast(I32), 0)
         vs_pool = sb.tile([P, T], F32, name="vs_pool")
-        nc.vector.memset(vs_pool[:], 0.0)
+        nc.vector.memset(vs_pool[:, : T // 2], 0.0)
         ks = sb.tile([P, PASSES, N], U8, name="ks", align_bytes=64)
         nc.vector.memset(ks[:].bitcast(I32), 0)
 
@@ -52,6 +52,7 @@ def tile_attend_qpk_topk_kernel(tc, q_words, q_scales, k_words, k_scales, vT, vs
         make_identity(nc, ident[:])
         minus_one = sb.tile([P, 1], F32, name="minus_one")
         nc.gpsimd.memset(minus_one[:], -1.0)
+        nc.gpsimd.memset(vs_pool[:, T // 2 :], 0.0)
 
         qw = sb.tile([P, PASSES, NQ], U32, name="qw", align_bytes=64)
         nc.sync.dma_start(qw[:].bitcast(I32), q_words[0].rearrange("o p q r -> p o (q r)").bitcast(I32))
@@ -112,7 +113,10 @@ def tile_attend_qpk_topk_kernel(tc, q_words, q_scales, k_words, k_scales, vT, vs
             v_t = ps.tile([P, 2, P], F32, name=f"v_t{h}", tag=bank)
             for u in range(2):
                 nc.tensor.transpose(v_t[:, u, :], v_g[:].bitcast(F32)[:, u::2], ident[:])
-            v_bf = sb.tile([P, P * 4], BF16, name=f"v_bf{h}", align_bytes=64)
+            return v_t
+
+        def interleave(h, v_t):
+            v_bf = late.tile([P, P * 4], BF16, name=f"v_bf{h}", offset=h * 1024, align_bytes=64)
             nc.scalar.copy(v_bf[:].bitcast(F32).rearrange("s (e u) -> s e u", u=2), v_t[:].rearrange("s u e -> s e u"))
             return v_bf
 
@@ -122,7 +126,7 @@ def tile_attend_qpk_topk_kernel(tc, q_words, q_scales, k_words, k_scales, vT, vs
             nc.vector.quantize_mx(codes[:].bitcast(FP8X4), scales[:], src[:])
             return codes, scales
 
-        v_bf = [values(0, "v_t0")]
+        v_t0 = values(0, "v_t0")
         p_t = []
         inv = []
         for b in range(QB):
@@ -142,7 +146,7 @@ def tile_attend_qpk_topk_kernel(tc, q_words, q_scales, k_words, k_scales, vT, vs
             nc.gpsimd.tensor_tensor(total[:], sums[:, 0:1], sums[:, 1:2], ALU.add)
             inv.append(sb.tile([P, 1], F32, name=f"inv{b}"))
             nc.gpsimd.tensor_tensor(inv[b][:], total[:], minus_one[:], ALU.pow)
-        v_bf.append(values(1, "score1"))
+        v_bf = [interleave(0, v_t0), interleave(1, values(1, "score1"))]
 
         w_bf = []
         for b in range(QB):

@@ -13,14 +13,19 @@ FP8X4 = mybir.dt.float8_e4m3fn_x4
 FP4X4 = mybir.dt.float4_e2m1fn_x4
 ACT = mybir.ActivationFunctionType
 ALU = mybir.AluOpType
+AXIS_X = mybir.AxisListType.X
 
 P = 128
 NQ, N, T, D, DV = 256, 512, 2048, 1024, 256
-PASSES = D // 512
+PACK = 4
+PASSES = D // (P * PACK)
 QB = NQ // P
 VB = DV // P
+QUADS = 4
 VS_ROW = 16
-V_HEAD = 1024
+POOL_BYTES = 4 * T
+WORDS_BYTES = 2 * P * PACK
+LINE = 64
 
 FLOPS = 2 * NQ * N * D + 2 * NQ * N * DV
 
@@ -29,7 +34,7 @@ def tile_attend_qpk_topk_kernel(tc, q_words, q_scales, k_words, k_scales, vT, vs
     nc = tc.nc
     with ExitStack() as ctx:
         sb = ctx.enter_context(tc.tile_pool(name="sb", bufs=1))
-        late = ctx.enter_context(tc.tile_pool(name="late", bufs=1))
+        reuse = ctx.enter_context(tc.tile_pool(name="reuse", bufs=1))
         ps = ctx.enter_context(tc.psum_pool(name="ps", bufs=1))
 
         offsets = sb.tile([P, N // 16], U16, name="offsets")
@@ -40,24 +45,21 @@ def tile_attend_qpk_topk_kernel(tc, q_words, q_scales, k_words, k_scales, vT, vs
         qs = sb.tile([P, PASSES, NQ], U8, name="qs", align_bytes=64)
         nc.vector.memset(qs[:].bitcast(I32), 0)
         vs_pool = sb.tile([P, T], F32, name="vs_pool")
-        nc.vector.memset(vs_pool[:, : T // 2], 0.0)
+        nc.vector.memset(vs_pool[:], 0.0)
         ks = sb.tile([P, PASSES, N], U8, name="ks", align_bytes=64)
         nc.vector.memset(ks[:].bitcast(I32), 0)
 
-        warm = sb.tile([P, 1], F32, name="warm")
+        warm = sb.tile([P, 1], F32, name="warm", tag="warm_ident")
         nc.gpsimd.memset(warm[:], 0.0)
         warm_out = sb.tile([P, 1], F32, name="warm_out")
         nc.scalar.activation(warm_out[:], warm[:], ACT.Exp)
-        ident = sb.tile([P, P], F32, name="ident")
+        ident = sb.tile([P, P], F32, name="ident", tag="warm_ident")
         make_identity(nc, ident[:])
-        minus_one = sb.tile([P, 1], F32, name="minus_one")
-        nc.gpsimd.memset(minus_one[:], -1.0)
-        nc.gpsimd.memset(vs_pool[:, T // 2 :], 0.0)
 
         qw = sb.tile([P, PASSES, NQ], U32, name="qw", align_bytes=64)
         nc.sync.dma_start(qw[:].bitcast(I32), q_words[0].rearrange("o p q r -> p o (q r)").bitcast(I32))
         nc.sync.dma_start(ks_pool[0:P:4, :].bitcast(I32), k_scales.rearrange("o f t -> f o t").bitcast(I32))
-        for quad in range(4):
+        for quad in range(QUADS):
             nc.sync.dma_start(
                 qs[32 * quad : 32 * quad + 4, :, :].bitcast(I32),
                 q_scales[0, :, 4 * quad : 4 * quad + 4, :].rearrange("o f q -> f o q").bitcast(I32),
@@ -67,32 +69,29 @@ def tile_attend_qpk_topk_kernel(tc, q_words, q_scales, k_words, k_scales, vT, vs
         nc.sync.dma_start(kw_pool[:, : T // 2].bitcast(I32), kw_dram[:, : T // 2])
         nc.sync.dma_start(vs_pool[VS_ROW : VS_ROW + 1, :], vs[0:1, :])
         nc.sync.dma_start(kw_pool[:, T // 2 :].bitcast(I32), kw_dram[:, T // 2 :])
-        v_pool = [
-            late.tile([P, T], F32, name="v_pool0", offset=0),
-            late.tile([P, T], F32, name="v_pool1", offset=4 * T),
-        ]
-        nc.sync.dma_start(v_pool[0][:, :V_HEAD], vT[0:P, :V_HEAD])
+        v_pool = [reuse.tile([P, T], F32, name=f"v_pool{h}", offset=h * POOL_BYTES) for h in range(VB)]
+        nc.sync.dma_start(v_pool[0][:, : T // 2], vT[0:P, : T // 2])
 
         ks_rows = sb.tile([P, N], U8, name="ks_rows")
         nc.vector.tensor_copy(ks_rows[:], ks_pool[:].indirect(offsets[:]))
-        for quad in range(4):
+        for quad in range(QUADS):
             nc.sync.dma_start(
                 ks[32 * quad : 32 * quad + 4, :, :].bitcast(I32), ks_rows[32 * quad : 32 * quad + 32 : 4, :].bitcast(I32)
             )
-        nc.sync.dma_start(v_pool[0][:, V_HEAD:], vT[0:P, V_HEAD:])
+        nc.sync.dma_start(v_pool[0][:, T // 2 :], vT[0:P, T // 2 :])
         nc.sync.dma_start(v_pool[1][:], vT[P : 2 * P, :])
 
         vs_g = sb.tile([P, N], F32, name="vs_g")
         nc.vector.tensor_copy(vs_g[:], vs_pool[:].indirect(offsets[:]))
-        vs_col = sb.tile([P, 4], F32, name="vs_col")
-        nc.scalar.dma_start(vs_col[:], vs_g[VS_ROW : VS_ROW + 1, :].rearrange("r (s t) -> r s t", t=4))
+        vs_col = sb.tile([P, PACK], F32, name="vs_col")
+        nc.scalar.dma_start(vs_col[:], vs_g[VS_ROW : VS_ROW + 1, :].rearrange("r (s t) -> r s t", t=PACK))
 
         kw_pairs = sb.tile([P, N], U32, name="kw_pairs")
         nc.vector.tensor_copy(kw_pairs[:], kw_pool[:].indirect(offsets[:]))
         kw = [sb.tile([P, N], U16, name=f"kw{o}", align_bytes=64) for o in range(PASSES)]
-        halves = kw_pairs[:].bitcast(U16).rearrange("p (n o) -> p o n", o=PASSES)
+        by_pass = kw_pairs[:].bitcast(U16).rearrange("p (n o) -> p o n", o=PASSES)
         for o in range(PASSES):
-            nc.vector.tensor_copy(kw[o][:], halves[:, o, :])
+            nc.vector.tensor_copy(kw[o][:], by_pass[:, o, :])
 
         score = [ps.tile([P, N], F32, name=f"score{b}", tag=f"score{b}") for b in range(QB)]
         for b in range(QB):
@@ -107,7 +106,7 @@ def tile_attend_qpk_topk_kernel(tc, q_words, q_scales, k_words, k_scales, vT, vs
                     stop=(o == PASSES - 1),
                 )
 
-        def values(h, bank):
+        def turn_values(h, bank):
             v_g = sb.tile([P, N], BF16, name=f"v_g{h}")
             nc.vector.tensor_copy(v_g[:], v_pool[h][:].indirect(offsets[:]))
             v_t = ps.tile([P, 2, P], F32, name=f"v_t{h}", tag=bank)
@@ -115,8 +114,8 @@ def tile_attend_qpk_topk_kernel(tc, q_words, q_scales, k_words, k_scales, vT, vs
                 nc.tensor.transpose(v_t[:, u, :], v_g[:].bitcast(F32)[:, u::2], ident[:])
             return v_t
 
-        def interleave(h, v_t):
-            v_bf = late.tile([P, P * 4], BF16, name=f"v_bf{h}", offset=h * 1024, align_bytes=64)
+        def interleave_values(h, v_t):
+            v_bf = reuse.tile([P, P * PACK], BF16, name=f"v_bf{h}", offset=h * WORDS_BYTES, align_bytes=64)
             nc.scalar.copy(v_bf[:].bitcast(F32).rearrange("s (e u) -> s e u", u=2), v_t[:].rearrange("s u e -> s e u"))
             return v_bf
 
@@ -126,37 +125,38 @@ def tile_attend_qpk_topk_kernel(tc, q_words, q_scales, k_words, k_scales, vT, vs
             nc.vector.quantize_mx(codes[:].bitcast(FP8X4), scales[:], src[:])
             return codes, scales
 
-        v_t0 = values(0, "v_t0")
+        v_t0 = turn_values(0, "v_t0")
         p_t = []
-        inv = []
+        sums = sb.tile([P, QB, 2], F32, name="sums")
         for b in range(QB):
-            neg_max = late.tile([P, 1], F32, name=f"neg_max{b}", offset=b * 64)
-            nc.vector.tensor_reduce(neg_max[:], score[b][:], mybir.AxisListType.X, ALU.max, negate=True)
-            p = sb.tile([P, 4, P], F32, name=f"p{b}")
-            sums = sb.tile([P, 2], F32, name=f"sums{b}")
-            dealt = score[b][:].rearrange("q (s t) -> q t s", t=4)
-            p_t.append(ps.tile([P, 4, P], F32, name=f"p_t{b}", tag=f"p_t{b}"))
-            for u in range(2):
+            neg_max = reuse.tile([P, 1], F32, name=f"neg_max{b}", offset=b * LINE)
+            nc.vector.tensor_reduce(neg_max[:], score[b][:], AXIS_X, ALU.max, negate=True)
+            p = sb.tile([P, PACK, P], F32, name=f"p{b}")
+            dealt = score[b][:].rearrange("q (s t) -> q t s", t=PACK)
+            p_t.append(ps.tile([P, PACK, P], F32, name=f"p_t{b}", tag=f"p_t{b}"))
+            for half in range(2):
+                places = slice(2 * half, 2 * half + 2)
                 nc.scalar.activation(
-                    p[:, 2 * u : 2 * u + 2, :], dealt[:, 2 * u : 2 * u + 2, :], ACT.Exp, bias=neg_max[:], accum_out=sums[:, u : u + 1]
+                    p[:, places, :], dealt[:, places, :], ACT.Exp, bias=neg_max[:], accum_out=sums[:, b, half : half + 1]
                 )
-                for t in range(2 * u, 2 * u + 2):
+                for t in range(places.start, places.stop):
                     nc.tensor.transpose(p_t[b][:, t, :], p[:, t, :], ident[:])
-            total = sb.tile([P, 1], F32, name=f"total{b}")
-            nc.gpsimd.tensor_tensor(total[:], sums[:, 0:1], sums[:, 1:2], ALU.add)
-            inv.append(sb.tile([P, 1], F32, name=f"inv{b}"))
-            nc.gpsimd.tensor_tensor(inv[b][:], total[:], minus_one[:], ALU.pow)
-        v_bf = [interleave(0, v_t0), interleave(1, values(1, "score1"))]
+        v_bf = [interleave_values(0, v_t0), interleave_values(1, turn_values(1, f"score{QB - 1}"))]
 
         w_bf = []
         for b in range(QB):
-            w_bf.append(late.tile([P, P * 4], BF16, name=f"w_bf{b}", offset=4 * T + b * 1024, align_bytes=64))
+            w_bf.append(reuse.tile([P, P * PACK], BF16, name=f"w_bf{b}", offset=POOL_BYTES + b * WORDS_BYTES, align_bytes=64))
             nc.vector.tensor_tensor(
-                w_bf[b][:].rearrange("s (q t) -> s q t", t=4),
+                w_bf[b][:].rearrange("s (q t) -> s q t", t=PACK),
                 p_t[b][:].rearrange("s t q -> s q t"),
-                vs_col[:].unsqueeze(1).to_broadcast([P, P, 4]),
+                vs_col[:].unsqueeze(1).to_broadcast([P, P, PACK]),
                 ALU.mult,
             )
+            if b == 0:
+                total = reuse.tile([P, QB], F32, name="total", offset=POOL_BYTES + QB * WORDS_BYTES)
+                nc.vector.tensor_reduce(total[:], sums[:], AXIS_X, ALU.add)
+        inv = sb.tile([P, QB], F32, name="inv")
+        nc.vector.reciprocal(inv[:], total[:])
 
         v_mx = [quantise(v_bf[0], "v0")]
         w_mx = [quantise(w_bf[b], f"w{b}") for b in range(QB)]
@@ -177,8 +177,8 @@ def tile_attend_qpk_topk_kernel(tc, q_words, q_scales, k_words, k_scales, vT, vs
                 res = sb.tile([P, P], F32, name=f"res{b}{h}")
                 dst = out[0, b * P : (b + 1) * P, h * P : (h + 1) * P]
                 if (b, h) == (QB - 1, VB - 1):
-                    nc.vector.tensor_scalar(res[:], y[:], inv[b][:], None, ALU.mult)
+                    nc.vector.tensor_scalar(res[:], y[:], inv[:, b : b + 1], None, ALU.mult)
                     nc.sync.dma_start(dst, res[:])
                 else:
-                    nc.scalar.activation(res[:], y[:], ACT.Copy, scale=inv[b][:])
+                    nc.scalar.activation(res[:], y[:], ACT.Copy, scale=inv[:, b : b + 1])
                     (nc.sync if h == 0 else nc.scalar).dma_start(dst, res[:])

from contextlib import ExitStack

import concourse.mybir as mybir
from concourse.masks import make_identity

F32 = mybir.dt.float32
BF16 = mybir.dt.bfloat16
I32 = mybir.dt.int32
U32 = mybir.dt.uint32
U16 = mybir.dt.uint16
U8 = mybir.dt.uint8
FP8X4 = mybir.dt.float8_e4m3fn_x4
FP4X4 = mybir.dt.float4_e2m1fn_x4
ACT = mybir.ActivationFunctionType
ALU = mybir.AluOpType
AXIS_X = mybir.AxisListType.X

P = 128
NQ, N, T, D, DV = 256, 512, 2048, 1024, 256
PACK = 4
PASSES = D // (P * PACK)
QB = NQ // P
VB = DV // P
QUADS = 4
VS_ROW = 16
POOL_BYTES = 4 * T
WORDS_BYTES = 2 * P * PACK
LINE = 64

FLOPS = 2 * NQ * N * D + 2 * NQ * N * DV


def tile_attend_qpk_topk_kernel(tc, q_words, q_scales, k_words, k_scales, vT, vs, offs, out):
    nc = tc.nc
    with ExitStack() as ctx:
        sb = ctx.enter_context(tc.tile_pool(name="sb", bufs=1))
        reuse = ctx.enter_context(tc.tile_pool(name="reuse", bufs=1))
        ps = ctx.enter_context(tc.psum_pool(name="ps", bufs=1))

        offsets = sb.tile([P, N // 16], U16, name="offsets")
        nc.sync.dma_start(offsets[:], offs)

        ks_pool = sb.tile([P, T], U8, name="ks_pool")
        nc.vector.memset(ks_pool[:].bitcast(I32), 0)
        qs = sb.tile([P, PASSES, NQ], U8, name="qs", align_bytes=64)
        nc.vector.memset(qs[:].bitcast(I32), 0)
        vs_pool = sb.tile([P, T], F32, name="vs_pool")
        nc.vector.memset(vs_pool[:], 0.0)
        ks = sb.tile([P, PASSES, N], U8, name="ks", align_bytes=64)
        nc.vector.memset(ks[:].bitcast(I32), 0)

        warm = sb.tile([P, 1], F32, name="warm", tag="warm_ident")
        nc.gpsimd.memset(warm[:], 0.0)
        warm_out = sb.tile([P, 1], F32, name="warm_out")
        nc.scalar.activation(warm_out[:], warm[:], ACT.Exp)
        ident = sb.tile([P, P], F32, name="ident", tag="warm_ident")
        make_identity(nc, ident[:])

        qw = sb.tile([P, PASSES, NQ], U32, name="qw", align_bytes=64)
        nc.sync.dma_start(qw[:].bitcast(I32), q_words[0].rearrange("o p q r -> p o (q r)").bitcast(I32))
        nc.sync.dma_start(ks_pool[0:P:4, :].bitcast(I32), k_scales.rearrange("o f t -> f o t").bitcast(I32))
        for quad in range(QUADS):
            nc.sync.dma_start(
                qs[32 * quad : 32 * quad + 4, :, :].bitcast(I32),
                q_scales[0, :, 4 * quad : 4 * quad + 4, :].rearrange("o f q -> f o q").bitcast(I32),
            )
        kw_pool = sb.tile([P, T], U32, name="kw_pool")
        kw_dram = k_words[0].rearrange("p t r -> p (t r)").bitcast(I32)
        nc.sync.dma_start(kw_pool[:, : T // 2].bitcast(I32), kw_dram[:, : T // 2])
        nc.sync.dma_start(vs_pool[VS_ROW : VS_ROW + 1, :], vs[0:1, :])
        nc.sync.dma_start(kw_pool[:, T // 2 :].bitcast(I32), kw_dram[:, T // 2 :])
        v_pool = [reuse.tile([P, T], F32, name=f"v_pool{h}", offset=h * POOL_BYTES) for h in range(VB)]
        nc.sync.dma_start(v_pool[0][:, : T // 2], vT[0:P, : T // 2])

        ks_rows = sb.tile([P, N], U8, name="ks_rows")
        nc.vector.tensor_copy(ks_rows[:], ks_pool[:].indirect(offsets[:]))
        for quad in range(QUADS):
            nc.sync.dma_start(
                ks[32 * quad : 32 * quad + 4, :, :].bitcast(I32), ks_rows[32 * quad : 32 * quad + 32 : 4, :].bitcast(I32)
            )
        nc.sync.dma_start(v_pool[0][:, T // 2 :], vT[0:P, T // 2 :])
        nc.sync.dma_start(v_pool[1][:], vT[P : 2 * P, :])

        vs_g = sb.tile([P, N], F32, name="vs_g")
        nc.vector.tensor_copy(vs_g[:], vs_pool[:].indirect(offsets[:]))
        vs_col = sb.tile([P, PACK], F32, name="vs_col")
        nc.scalar.dma_start(vs_col[:], vs_g[VS_ROW : VS_ROW + 1, :].rearrange("r (s t) -> r s t", t=PACK))

        kw_pairs = sb.tile([P, N], U32, name="kw_pairs")
        nc.vector.tensor_copy(kw_pairs[:], kw_pool[:].indirect(offsets[:]))
        kw = [sb.tile([P, N], U16, name=f"kw{o}", align_bytes=64) for o in range(PASSES)]
        by_pass = kw_pairs[:].bitcast(U16).rearrange("p (n o) -> p o n", o=PASSES)
        for o in range(PASSES):
            nc.vector.tensor_copy(kw[o][:], by_pass[:, o, :])

        score = [ps.tile([P, N], F32, name=f"score{b}", tag=f"score{b}") for b in range(QB)]
        for b in range(QB):
            for o in range(PASSES):
                nc.tensor.matmul_mx(
                    out=score[b][:],
                    lhsT=qw[:, o, b * P : (b + 1) * P].bitcast(FP8X4),
                    lhsT_scale=qs[:, o, b * P : (b + 1) * P],
                    rhs=kw[o][:].bitcast(FP4X4),
                    rhs_scale=ks[:, o, :],
                    start=(o == 0),
                    stop=(o == PASSES - 1),
                )

        def turn_values(h, bank):
            v_g = sb.tile([P, N], BF16, name=f"v_g{h}")
            nc.vector.tensor_copy(v_g[:], v_pool[h][:].indirect(offsets[:]))
            v_t = ps.tile([P, 2, P], F32, name=f"v_t{h}", tag=bank)
            for u in range(2):
                nc.tensor.transpose(v_t[:, u, :], v_g[:].bitcast(F32)[:, u::2], ident[:])
            return v_t

        def interleave_values(h, v_t):
            v_bf = reuse.tile([P, P * PACK], BF16, name=f"v_bf{h}", offset=h * WORDS_BYTES, align_bytes=64)
            nc.scalar.copy(v_bf[:].bitcast(F32).rearrange("s (e u) -> s e u", u=2), v_t[:].rearrange("s u e -> s e u"))
            return v_bf

        def quantise(src, name):
            codes = sb.tile([P, P], U32, name=f"{name}_codes", align_bytes=64)
            scales = sb.tile([P, P], U8, name=f"{name}_scales", align_bytes=64)
            nc.vector.quantize_mx(codes[:].bitcast(FP8X4), scales[:], src[:])
            return codes, scales

        v_t0 = turn_values(0, "v_t0")
        p_t = []
        sums = sb.tile([P, QB, 2], F32, name="sums")
        for b in range(QB):
            neg_max = reuse.tile([P, 1], F32, name=f"neg_max{b}", offset=b * LINE)
            nc.vector.tensor_reduce(neg_max[:], score[b][:], AXIS_X, ALU.max, negate=True)
            p = sb.tile([P, PACK, P], F32, name=f"p{b}")
            dealt = score[b][:].rearrange("q (s t) -> q t s", t=PACK)
            p_t.append(ps.tile([P, PACK, P], F32, name=f"p_t{b}", tag=f"p_t{b}"))
            for half in range(2):
                places = slice(2 * half, 2 * half + 2)
                nc.scalar.activation(
                    p[:, places, :], dealt[:, places, :], ACT.Exp, bias=neg_max[:], accum_out=sums[:, b, half : half + 1]
                )
                for t in range(places.start, places.stop):
                    nc.tensor.transpose(p_t[b][:, t, :], p[:, t, :], ident[:])
        v_bf = [interleave_values(0, v_t0), interleave_values(1, turn_values(1, f"score{QB - 1}"))]

        w_bf = []
        for b in range(QB):
            w_bf.append(reuse.tile([P, P * PACK], BF16, name=f"w_bf{b}", offset=POOL_BYTES + b * WORDS_BYTES, align_bytes=64))
            nc.vector.tensor_tensor(
                w_bf[b][:].rearrange("s (q t) -> s q t", t=PACK),
                p_t[b][:].rearrange("s t q -> s q t"),
                vs_col[:].unsqueeze(1).to_broadcast([P, P, PACK]),
                ALU.mult,
            )
            if b == 0:
                total = reuse.tile([P, QB], F32, name="total", offset=POOL_BYTES + QB * WORDS_BYTES)
                nc.vector.tensor_reduce(total[:], sums[:], AXIS_X, ALU.add)
        inv = sb.tile([P, QB], F32, name="inv")
        nc.vector.reciprocal(inv[:], total[:])

        v_mx = [quantise(v_bf[0], "v0")]
        w_mx = [quantise(w_bf[b], f"w{b}") for b in range(QB)]
        v_mx.append(quantise(v_bf[1], "v1"))

        for h in range(VB):
            for b in range(QB):
                y = ps.tile([P, P], F32, name=f"y{b}{h}", tag=f"y{b}" if h == 0 else f"p_t{b}")
                nc.tensor.matmul_mx(
                    out=y[:],
                    lhsT=w_mx[b][0][:].bitcast(FP8X4),
                    lhsT_scale=w_mx[b][1][:],
                    rhs=v_mx[h][0][:].bitcast(FP8X4),
                    rhs_scale=v_mx[h][1][:],
                    start=True,
                    stop=True,
                )
                res = sb.tile([P, P], F32, name=f"res{b}{h}")
                dst = out[0, b * P : (b + 1) * P, h * P : (h + 1) * P]
                if (b, h) == (QB - 1, VB - 1):
                    nc.vector.tensor_scalar(res[:], y[:], inv[:, b : b + 1], None, ALU.mult)
                    nc.sync.dma_start(dst, res[:])
                else:
                    nc.scalar.activation(res[:], y[:], ACT.Copy, scale=inv[:, b : b + 1])
                    (nc.sync if h == 0 else nc.scalar).dma_start(dst, res[:])
